import numpy as np
import ml_dtypes


def mxq(x, axis, fmt="e4m3"):
    dtype, down = {"e4m3": (ml_dtypes.float8_e4m3fn, 7), "e5m2": (ml_dtypes.float8_e5m2, 14)}[fmt]
    v = np.moveaxis(np.asarray(x, np.float32).astype(ml_dtypes.bfloat16).astype(np.float64), axis, -1)
    blocks = v.reshape(v.shape[:-1] + (-1, 32))
    amax = np.abs(blocks).max(-1, keepdims=True)
    byte = np.maximum(np.where(amax > 0, np.frexp(amax)[1] - 1 + 127, 0) - down, 1)
    scale = np.exp2(byte - 127.0)
    codes = (blocks / scale).astype(np.float32).astype(dtype).astype(np.float64)
    return np.moveaxis((codes * scale).reshape(v.shape), -1, axis)


WIDE = False


def mx_kscale(k):
    if not WIDE:
        return np.ones(k)
    levels = np.array([10, -10, 5, -5, 0])
    if k % 512:
        return np.exp2(np.random.permutation(np.resize(levels, k // 32))).repeat(32)
    a = np.empty((k // 512, 16))
    for p in range(k // 512):
        a[p, :8] = np.random.permutation(np.resize(levels, 8))
        for g in range(8):
            far = levels[np.abs(levels - a[p, g]) >= 10]
            a[p, g + 8] = far[np.random.randint(len(far))]
    return np.exp2(a.ravel()).repeat(32)


def f64(x):
    return np.asarray(x).astype(np.float64)


def striped(idx):
    return np.tile(np.asarray(idx).reshape(-1, 16).T, (8, 1)).astype(np.uint16)


def unstriped(offs):
    return offs[:16].T.reshape(-1).astype(np.int64)


E2M1 = np.array([0.0, 0.5, 1.0, 1.5, 2.0, 3.0, 4.0, 6.0, -0.0, -0.5, -1.0, -1.5, -2.0, -3.0, -4.0, -6.0])


def pack_weight(w, fmt):
    k, n = w.shape
    w = f64(np.asarray(w, np.float32).astype(ml_dtypes.bfloat16)).reshape(k // 32, 32, n)
    amax = np.abs(w).max(1)
    if fmt == "e4m3":
        byte = np.frexp(amax)[1] - 1 + 127 - 7
    else:
        mant, ex = np.frexp(amax / 6.0)
        byte = np.where(mant > 0.5, ex, ex - 1) + 127
    byte = np.clip(np.where(amax > 0, byte, 1), 1, 254)
    scaled = (w * np.exp2(127.0 - byte)[:, None, :]).reshape(k, n).astype(np.float32)
    by_word = np.ascontiguousarray(scaled.reshape(k // 512, 128, 4, n).transpose(0, 1, 3, 2))
    if fmt == "e4m3":
        words = by_word.astype(ml_dtypes.float8_e4m3fn).view(np.uint8)
    else:
        c = by_word.astype(ml_dtypes.float4_e2m1fn).view(np.uint8) & 0xF
        words = (c[..., 0::2] | (c[..., 1::2] << 4)).reshape(k // 512, 128, 2 * n)
    return np.ascontiguousarray(words), np.ascontiguousarray(byte.astype(np.uint8).reshape(k // 512, 16, n))


def unpack_weight(words, scales, fmt):
    g, _, n = scales.shape
    words = np.ascontiguousarray(words).reshape(g, 128, n, -1)
    if fmt == "e4m3":
        vals = words.view(ml_dtypes.float8_e4m3fn).astype(np.float64)
    else:
        nib = np.empty((g, 128, n, 4), np.uint8)
        nib[..., 0::2] = words & 0xF
        nib[..., 1::2] = words >> 4
        vals = E2M1[nib]
    vals = vals * np.repeat(np.exp2(scales.astype(np.float64) - 127.0), 8, axis=1)[..., None]
    return vals.transpose(0, 1, 3, 2).reshape(g * 512, n)


def bf(x):
    return np.asarray(x, np.float32).astype(ml_dtypes.bfloat16)


def planes(Y):
    r, m = Y.shape
    b = f64(bf(Y)).reshape(r // 32, 32, m)
    amax = np.abs(b).max(1)
    byte = np.clip(np.where(amax > 0, np.frexp(amax)[1] - 1 + 127 - 7, 1), 1, 254)
    codes = (b * np.exp2(127.0 - byte)[:, None, :]).reshape(r, m).astype(np.float32).astype(ml_dtypes.float8_e4m3fn).view(np.uint8)
    words = codes.reshape(r // 512, 128, 4, m).transpose(0, 1, 3, 2)
    return np.ascontiguousarray(words), np.ascontiguousarray(byte.astype(np.uint8).reshape(r // 512, 16, m))


D, E, T, I, Q, G = 512, 512, 1024, 256, 512, 16


def setup_inputs():
    n = np.random.standard_normal
    idx = np.random.permutation(T)[:I]
    fd = mx_kscale(D)
    fq = mx_kscale(Q)
    keysp = pack_weight(n((D, T)) / fd[:, None], "e4m3")
    return {
        "query": (n((D, Q)) * 0.5 / np.sqrt(D) * fd[:, None]).astype(np.float32),
        "qs": (np.random.uniform(8.0, 32.0, (Q, 1)) * fq[:, None]).astype(np.float32),
        "grows": (n((Q, E)) / fq[:, None]).astype(np.float32),
        "vals": (n((E, T))).astype(np.float32),
        "keys_words": keysp[0],
        "keys_scales": keysp[1],
        "share": (np.random.uniform(0.4, 1.0, (E, 1))).astype(np.float32),
        "pre": (np.random.uniform(0.6, 1.6, (1, I))).astype(np.float32),
        "sg": (np.random.uniform(0.5, 2.0, (1, I))).astype(np.float32),
        "old": (0.5 * n((E, I))).astype(np.float32),
        "offs": striped(idx),
    }


def reference(query, qs, grows, vals, keys_words, keys_scales, share, pre, sg, old, offs):
    idx = unstriped(offs)
    keysu = unpack_weight(keys_words, keys_scales, "e4m3")
    queryq = mxq(f64(query), 0, "e4m3")
    keysidxg = keysu[:, idx]
    a = queryq.T @ keysidxg
    p = np.exp(a - np.max(a, axis=1, keepdims=True))
    w = p * f64(qs) / np.sum(p, axis=1, keepdims=True)
    growsq = mxq(f64(grows), 0, "e4m3")
    wq = mxq(w, 0, "e4m3")
    c0 = growsq.T @ wq
    x1 = f64(vals)[:, idx] * f64(pre)
    m1 = x1.reshape(E, G, I // G).mean(axis=2)
    mr = np.repeat(m1, I // G, axis=1)
    x2 = x1 - mr * f64(share)
    vp = np.tanh(x2)
    dx2 = c0 * (1.0 - np.square(vp))
    dmr = dx2 * (-1.0) * f64(share)
    dm1 = dmr.reshape(E, G, I // G).sum(axis=2)
    e1 = dm1 / 16.0
    r1 = np.repeat(e1, I // G, axis=1)
    dx1 = dx2 + r1
    y = dx1 * f64(sg) + f64(old)
    words, scales = planes(y)
    return y, words, scales

@@ -1,0 +1,275 @@
+from contextlib import ExitStack
+
+import concourse.mybir as mybir
+from concourse.masks import make_identity
+
+D, E, T, I, Q, G = 512, 512, 1024, 256, 512, 16
+FLOPS = 2 * D * Q * I + 2 * Q * E * I
+
+F32 = mybir.dt.float32
+BF16 = mybir.dt.bfloat16
+I32 = mybir.dt.int32
+U32 = mybir.dt.uint32
+U16 = mybir.dt.uint16
+U8 = mybir.dt.uint8
+FP8X4 = mybir.dt.float8_e4m3fn_x4
+ALU = mybir.AluOpType
+ACT = mybir.ActivationFunctionType
+AX = mybir.AxisListType
+
+P = 128
+PACK = 4
+PAGE = I // G
+HALF = I // 2
+
+
+def tile_attend_bvpagecentred_d_pl_kernel(
+    tc, query, qs, grows, vals, keys_words, keys_scales, share, pre, sg, old, offs, out_0, out_1, out_2
+):
+    nc = tc.nc
+    with ExitStack() as ctx:
+        sb = ctx.enter_context(tc.tile_pool(name="sb", bufs=1))
+        ps = ctx.enter_context(tc.psum_pool(name="ps", bufs=1))
+
+        def deal_cast(engine_copy, grouped, raw, h):
+            engine_copy(
+                out=grouped[:, :, 64 * h : 64 * (h + 1), :].rearrange("p r s j -> p s r j"),
+                in_=raw[:].rearrange("p j (s r) -> p s r j", r=PACK),
+            )
+
+        offsets = sb.tile([P, I // 16], U16, name="offsets")
+        nc.sync.dma_start(offsets[:], offs)
+
+        key_words = sb.tile([P, T], I32, name="key_words", align_bytes=64)
+        nc.sync.dma_start(key_words[:], keys_words[0].rearrange("p n t -> p (n t)").bitcast(I32))
+
+        key_bytes = sb.tile([P, T], U8, name="key_bytes", align_bytes=64)
+        nc.vector.memset(key_bytes[:].bitcast(I32), 0)
+        for quad in range(4):
+            nc.scalar.dma_start(
+                key_bytes[32 * quad : 32 * quad + 4, :].bitcast(I32),
+                keys_scales[0, 4 * quad : 4 * quad + 4, :].bitcast(I32),
+            )
+
+        warm = sb.tile([P, 1], F32, name="warm")
+        warm_out = sb.tile([P, 1], F32, name="warm_out")
+        nc.vector.memset(warm[:], 0.0)
+        nc.scalar.activation(out=warm_out[:], in_=warm[:], func=ACT.Exp)
+
+        ident = sb.tile([P, P], F32, name="ident")
+        make_identity(nc, ident[:])
+
+        pre_col = sb.tile([P, 2], F32, name="pre_col")
+        share_col = sb.tile([P, PACK], F32, name="share_col")
+        sg_col = sb.tile([P, 2], F32, name="sg_col")
+        qs_col = sb.tile([P, PACK], F32, name="qs_col")
+        nc.sync.dma_start(pre_col[:], pre.rearrange("o (p c) -> (o p) c", c=2))
+
+        query_rows = query.rearrange("(p j) q -> p j q", j=PACK)
+        grows_rows = grows.rearrange("(p j) e -> p j e", j=PACK)
+        vals_rows = vals.rearrange("(p t) n -> p t n", t=PACK)
+        q_raw = [sb.tile([P, PACK, Q // 2], F32, name="q_raw%d" % h) for h in range(2)]
+        g_raw = [sb.tile([P, PACK, E // 2], F32, name="g_raw%d" % h) for h in range(2)]
+        v_pool = [sb.tile([P, T], F32, name="v_pool%d" % t) for t in range(PACK)]
+        old_sb = sb.tile([P, PACK, I], F32, name="old_sb")
+        for h in range(2):
+            nc.sync.dma_start(q_raw[h][:], query_rows[:, :, 256 * h : 256 * (h + 1)])
+        nc.sync.dma_start(share_col[:], share.rearrange("(p t) o -> p (t o)", t=PACK))
+        for t in (0, 1):
+            nc.sync.dma_start(v_pool[t][:], vals_rows[:, t, :])
+        nc.sync.dma_start(qs_col[:], qs.rearrange("(p t) o -> p (t o)", t=PACK))
+        for h in range(2):
+            nc.sync.dma_start(g_raw[h][:], grows_rows[:, :, 256 * h : 256 * (h + 1)])
+        nc.sync.dma_start(sg_col[:], sg.rearrange("o (p c) -> (o p) c", c=2))
+        for t in (2, 3):
+            nc.sync.dma_start(v_pool[t][:], vals_rows[:, t, :])
+        nc.sync.dma_start(old_sb[:], old.rearrange("(p t) i -> p t i", t=PACK))
+
+        def spread(col, name):
+            bank = ps.tile([P, 2, P], F32, name=name + "_bank")
+            for c in range(2):
+                nc.tensor.transpose(bank[:, c, :], col[:, c : c + 1].to_broadcast([P, P]), ident[:])
+            row = sb.tile([P, I], F32, name=name + "_row")
+            nc.scalar.copy(out=row[:].rearrange("p (n c) -> p n c", c=2), in_=bank[:].rearrange("p c n -> p n c"))
+            return row
+
+        pre_row = spread(pre_col, "pre")
+        sg_row = spread(sg_col, "sg")
+        share16 = sb.tile([P, PACK], F32, name="share16")
+        nshare16 = sb.tile([P, PACK], F32, name="nshare16")
+        nc.scalar.activation(out=share16[:], in_=share_col[:], func=ACT.Copy, scale=1.0 / PAGE)
+        nc.scalar.activation(out=nshare16[:], in_=share_col[:], func=ACT.Copy, scale=-1.0 / PAGE)
+
+        k_words = sb.tile([P, I], U32, name="k_words", align_bytes=64)
+        k_bytes = sb.tile([P, I], U8, name="k_bytes", align_bytes=64)
+        nc.vector.tensor_copy(k_words[:], key_words[:].bitcast(U32).indirect(offsets[:]))
+        nc.vector.tensor_copy(k_bytes[:], key_bytes[:].indirect(offsets[:]))
+
+        q_bf = sb.tile([P, PACK, P, PACK], BF16, name="q_bf", align_bytes=64)
+        deal_cast(nc.scalar.copy, q_bf, q_raw[0], 0)
+        deal_cast(nc.vector.tensor_copy, q_bf, q_raw[1], 1)
+        q_codes = sb.tile([P, Q], U32, name="q_codes", align_bytes=64)
+        q_scales = sb.tile([P, Q], U8, name="q_scales", align_bytes=64)
+        nc.vector.quantize_mx(
+            out=q_codes[:].bitcast(FP8X4), scales=q_scales[:], in_=q_bf[:].rearrange("p r s j -> p (r s j)")
+        )
+
+        neg_max = sb.tile([P, PACK], F32, name="neg_max")
+        sums = sb.tile([P, PACK], F32, name="sums")
+        probs = sb.tile([P, PACK, I], F32, name="probs")
+        for r in range(PACK):
+            cols = slice(P * r, P * (r + 1))
+            scores = ps.tile([P, I], F32, name="scores%d" % r)
+            nc.tensor.matmul_mx(
+                out=scores[:],
+                lhsT=q_codes[:, cols].bitcast(FP8X4),
+                lhsT_scale=q_scales[:, cols],
+                rhs=k_words[:].bitcast(FP8X4),
+                rhs_scale=k_bytes[:],
+                start=True,
+                stop=True,
+            )
+            nc.vector.tensor_reduce(out=neg_max[:, r : r + 1], in_=scores[:], axis=AX.X, op=ALU.max, negate=True)
+            nc.scalar.activation(
+                out=probs[:, r, :],
+                in_=scores[:],
+                func=ACT.Exp,
+                bias=neg_max[:, r : r + 1],
+                scale=1.0,
+                accum_out=sums[:, r : r + 1],
+            )
+
+        sq = sb.tile([P, PACK, I], F32, name="sq")
+
+        def prepare_plane(t):
+            x1 = sb.tile([P, I], F32, name="x1_%d" % t)
+            nc.vector.tensor_tensor(x1[:], v_pool[t][:].indirect(offsets[:]), pre_row[:], ALU.mult)
+            page_sum = sb.tile([P, G], F32, name="page_sum%d" % t)
+            nc.vector.tensor_reduce(
+                out=page_sum[:], in_=x1[:].rearrange("p (g k) -> p g k", k=PAGE), axis=AX.X, op=ALU.add
+            )
+            x2 = sb.tile([P, I], F32, name="x2_%d" % t)
+            nc.vector.scalar_tensor_tensor(
+                out=x2[:].rearrange("p (g k) -> p g k", k=PAGE),
+                in0=page_sum[:].unsqueeze(2).to_broadcast([P, G, PAGE]),
+                scalar=nshare16[:, t : t + 1],
+                in1=x1[:].rearrange("p (g k) -> p g k", k=PAGE),
+                op0=ALU.mult,
+                op1=ALU.add,
+            )
+            vp = sb.tile([P, I], F32, name="vp_%d" % t)
+            nc.scalar.activation(out=vp[:], in_=x2[:], func=ACT.Tanh)
+            nc.scalar.activation(out=sq[:, t, :], in_=vp[:], func=ACT.Square)
+
+        prepare_plane(0)
+        prepare_plane(1)
+
+        inv = sb.tile([P, PACK], F32, name="inv")
+        nc.vector.reciprocal(out=inv[:], in_=sums[:])
+        w_planes = sb.tile([P, PACK, I], BF16, name="w_planes", align_bytes=64)
+        for r in range(PACK):
+            nc.vector.tensor_scalar(
+                out=w_planes[:, r, :],
+                in0=probs[:, r, :],
+                scalar1=qs_col[:, r : r + 1],
+                scalar2=inv[:, r : r + 1],
+                op0=ALU.mult,
+                op1=ALU.mult,
+            )
+        w_bf = sb.tile([P, I, PACK], BF16, name="w_bf", align_bytes=64)
+        nc.vector.tensor_copy(
+            out=w_bf[:].rearrange("p (c i) r -> p c r i", i=4),
+            in_=w_planes[:].rearrange("p r (c i) -> p c r i", i=4),
+        )
+        w_codes = sb.tile([P, I], U32, name="w_codes", align_bytes=64)
+        w_scales = sb.tile([P, I], U8, name="w_scales", align_bytes=64)
+        nc.vector.quantize_mx(
+            out=w_codes[:].bitcast(FP8X4), scales=w_scales[:], in_=w_bf[:].rearrange("p i r -> p (i r)")
+        )
+
+        g_bf = sb.tile([P, PACK, P, PACK], BF16, name="g_bf", align_bytes=64)
+        deal_cast(nc.scalar.copy, g_bf, g_raw[0], 0)
+        deal_cast(nc.scalar.copy, g_bf, g_raw[1], 1)
+        g_codes = sb.tile([P, E], U32, name="g_codes", align_bytes=64)
+        g_scales = sb.tile([P, E], U8, name="g_scales", align_bytes=64)
+        nc.vector.quantize_mx(
+            out=g_codes[:].bitcast(FP8X4), scales=g_scales[:], in_=g_bf[:].rearrange("p r s j -> p (r s j)")
+        )
+
+        c0 = [ps.tile([P, PACK, HALF], F32, name="c0_%d" % h) for h in range(2)]
+        for h in range(2):
+            slots = slice(HALF * h, HALF * (h + 1))
+            for t in range(PACK):
+                cols = slice(P * t, P * (t + 1))
+                nc.tensor.matmul_mx(
+                    out=c0[h][:, t, :],
+                    lhsT=g_codes[:, cols].bitcast(FP8X4),
+                    lhsT_scale=g_scales[:, cols],
+                    rhs=w_codes[:, slots].bitcast(FP8X4),
+                    rhs_scale=w_scales[:, slots],
+                    start=True,
+                    stop=True,
+                )
+
+        prepare_plane(2)
+        prepare_plane(3)
+
+        halves = [slice(HALF * h, HALF * (h + 1)) for h in range(2)]
+        ndx2 = [sb.tile([P, PACK, HALF], F32, name="ndx2_%d" % h) for h in range(2)]
+        back_sum = [sb.tile([P, PACK, G // 2], F32, name="back_sum%d" % h) for h in range(2)]
+        dx1 = [sb.tile([P, PACK, HALF], F32, name="dx1_%d" % h) for h in range(2)]
+        gained = [sb.tile([P, PACK, HALF], F32, name="gained%d" % h) for h in range(2)]
+        y = [sb.tile([P, PACK, HALF], F32, name="y%d" % h) for h in range(2)]
+        y_bf = [sb.tile([P, HALF, PACK], BF16, name="y_bf%d" % h, align_bytes=64) for h in range(2)]
+        y_codes = sb.tile([P, I], U32, name="y_codes", align_bytes=64)
+        y_scales = sb.tile([P, I], U8, name="y_scales", align_bytes=64)
+        for h in range(2):
+            nc.vector.scalar_tensor_tensor(
+                out=ndx2[h][:], in0=sq[:, :, halves[h]], scalar=1.0, in1=c0[h][:], op0=ALU.subtract, op1=ALU.mult
+            )
+        for h in range(2):
+            nc.vector.tensor_reduce(
+                out=back_sum[h][:].rearrange("p t g -> p (t g)"),
+                in_=ndx2[h][:].rearrange("p t (g k) -> p (t g) k", k=PAGE),
+                axis=AX.X,
+                op=ALU.add,
+            )
+        for h in range(2):
+            for t in range(PACK):
+                nc.vector.scalar_tensor_tensor(
+                    out=dx1[h][:, t, :].rearrange("p (g k) -> p g k", k=PAGE),
+                    in0=back_sum[h][:, t, :].unsqueeze(2).to_broadcast([P, G // 2, PAGE]),
+                    scalar=share16[:, t : t + 1],
+                    in1=ndx2[h][:, t, :].rearrange("p (g k) -> p g k", k=PAGE),
+                    op0=ALU.mult,
+                    op1=ALU.subtract,
+                )
+        for h in range(2):
+            nc.vector.tensor_tensor(
+                out=gained[h][:],
+                in0=dx1[h][:],
+                in1=sg_row[:, halves[h]].unsqueeze(1).to_broadcast([P, PACK, HALF]),
+                op=ALU.mult,
+            )
+        out_rows = out_0.rearrange("(p t) i -> p t i", t=PACK)
+        for h in range(2):
+            nc.vector.tensor_tensor(out=y[h][:], in0=gained[h][:], in1=old_sb[:, :, halves[h]], op=ALU.add)
+            nc.sync.dma_start(out_rows[:, :, halves[h]], y[h][:])
+        for h, engine_copy in ((0, nc.scalar.copy), (1, nc.vector.tensor_copy)):
+            engine_copy(
+                out=y_bf[h][:].rearrange("p (c i) t -> p c t i", i=4),
+                in_=y[h][:].rearrange("p t (c i) -> p c t i", i=4),
+            )
+        for h in range(2):
+            nc.vector.quantize_mx(
+                out=y_codes[:, halves[h]].bitcast(FP8X4),
+                scales=y_scales[:, halves[h]],
+                in_=y_bf[h][:].rearrange("p i t -> p (i t)"),
+            )
+        nc.sync.dma_start(out_1[0].rearrange("p n t -> p (n t)").bitcast(I32), y_codes[:].bitcast(I32))
+        for quad in range(4):
+            queue = nc.sync if quad % 2 == 0 else nc.scalar
+            queue.dma_start(
+                out_2[0, 4 * quad : 4 * quad + 4, :].bitcast(I32),
+                y_scales[32 * quad : 32 * quad + 4, :].bitcast(I32),
+            )

@@ -20,7 +20,6 @@ AX = mybir.AxisListType
 P = 128
 PACK = 4
 PAGE = I // G
-HALF = I // 2
 
 
 def tile_attend_bvpagecentred_d_pl_kernel(
@@ -31,97 +30,114 @@ def tile_attend_bvpagecentred_d_pl_kernel(
         sb = ctx.enter_context(tc.tile_pool(name="sb", bufs=1))
         ps = ctx.enter_context(tc.psum_pool(name="ps", bufs=1))
 
-        def deal_cast(engine_copy, grouped, raw, h):
+        def deal_cast(engine_copy, grouped, raw, s0, s1):
             engine_copy(
-                out=grouped[:, :, 64 * h : 64 * (h + 1), :].rearrange("p r s j -> p s r j"),
-                in_=raw[:].rearrange("p j (s r) -> p s r j", r=PACK),
+                out=grouped[:, :, s0:s1, :].rearrange("p r s j -> p s r j"),
+                in_=raw[:, :, PACK * s0 : PACK * s1].rearrange("p j (s r) -> p s r j", r=PACK),
             )
+
+        def paged(ap):
+            return ap.rearrange("p (g k) -> p g k", k=PAGE)
 
         offsets = sb.tile([P, I // 16], U16, name="offsets")
-        nc.sync.dma_start(offsets[:], offs)
-
         key_words = sb.tile([P, T], I32, name="key_words", align_bytes=64)
-        nc.sync.dma_start(key_words[:], keys_words[0].rearrange("p n t -> p (n t)").bitcast(I32))
-
         key_bytes = sb.tile([P, T], U8, name="key_bytes", align_bytes=64)
-        nc.vector.memset(key_bytes[:].bitcast(I32), 0)
-        for quad in range(4):
-            nc.scalar.dma_start(
-                key_bytes[32 * quad : 32 * quad + 4, :].bitcast(I32),
-                keys_scales[0, 4 * quad : 4 * quad + 4, :].bitcast(I32),
-            )
-
-        warm = sb.tile([P, 1], F32, name="warm")
-        warm_out = sb.tile([P, 1], F32, name="warm_out")
-        nc.vector.memset(warm[:], 0.0)
-        nc.scalar.activation(out=warm_out[:], in_=warm[:], func=ACT.Exp)
-
-        ident = sb.tile([P, P], F32, name="ident")
-        make_identity(nc, ident[:])
-
         pre_col = sb.tile([P, 2], F32, name="pre_col")
         share_col = sb.tile([P, PACK], F32, name="share_col")
         sg_col = sb.tile([P, 2], F32, name="sg_col")
         qs_col = sb.tile([P, PACK], F32, name="qs_col")
-        nc.sync.dma_start(pre_col[:], pre.rearrange("o (p c) -> (o p) c", c=2))
-
         query_rows = query.rearrange("(p j) q -> p j q", j=PACK)
         grows_rows = grows.rearrange("(p j) e -> p j e", j=PACK)
         vals_rows = vals.rearrange("(p t) n -> p t n", t=PACK)
-        q_raw = [sb.tile([P, PACK, Q // 2], F32, name="q_raw%d" % h) for h in range(2)]
-        g_raw = [sb.tile([P, PACK, E // 2], F32, name="g_raw%d" % h) for h in range(2)]
+        old_rows = old.rearrange("(p t) i -> p t i", t=PACK)
+        out_rows = out_0.rearrange("(p t) i -> p t i", t=PACK)
+        q_raw = sb.tile([P, PACK, Q], F32, name="q_raw")
+        g_raw = sb.tile([P, PACK, E], F32, name="g_raw")
         v_pool = [sb.tile([P, T], F32, name="v_pool%d" % t) for t in range(PACK)]
         old_sb = sb.tile([P, PACK, I], F32, name="old_sb")
-        for h in range(2):
-            nc.sync.dma_start(q_raw[h][:], query_rows[:, :, 256 * h : 256 * (h + 1)])
-        nc.sync.dma_start(share_col[:], share.rearrange("(p t) o -> p (t o)", t=PACK))
-        for t in (0, 1):
-            nc.sync.dma_start(v_pool[t][:], vals_rows[:, t, :])
-        nc.sync.dma_start(qs_col[:], qs.rearrange("(p t) o -> p (t o)", t=PACK))
-        for h in range(2):
-            nc.sync.dma_start(g_raw[h][:], grows_rows[:, :, 256 * h : 256 * (h + 1)])
-        nc.sync.dma_start(sg_col[:], sg.rearrange("o (p c) -> (o p) c", c=2))
-        for t in (2, 3):
-            nc.sync.dma_start(v_pool[t][:], vals_rows[:, t, :])
-        nc.sync.dma_start(old_sb[:], old.rearrange("(p t) i -> p t i", t=PACK))
 
-        def spread(col, name):
-            bank = ps.tile([P, 2, P], F32, name=name + "_bank")
-            for c in range(2):
-                nc.tensor.transpose(bank[:, c, :], col[:, c : c + 1].to_broadcast([P, P]), ident[:])
-            row = sb.tile([P, I], F32, name=name + "_row")
-            nc.scalar.copy(out=row[:].rearrange("p (n c) -> p n c", c=2), in_=bank[:].rearrange("p c n -> p n c"))
-            return row
+        def load_offs():
+            nc.sync.dma_start(offsets[:], offs)
 
-        pre_row = spread(pre_col, "pre")
-        sg_row = spread(sg_col, "sg")
+        def load_kw():
+            nc.sync.dma_start(key_words[:], keys_words[0].rearrange("p n t -> p (n t)").bitcast(I32))
+
+        def load_ks():
+            for quad in range(4):
+                nc.sync.dma_start(
+                    key_bytes[32 * quad : 32 * quad + 4, :].bitcast(I32),
+                    keys_scales[0, 4 * quad : 4 * quad + 4, :].bitcast(I32),
+                )
+
+        def load_pre():
+            nc.sync.dma_start(pre_col[:], pre.rearrange("o (p c) -> (o p) c", c=2))
+
+        def load_sg():
+            nc.sync.dma_start(sg_col[:], sg.rearrange("o (p c) -> (o p) c", c=2))
+
+        def load_share():
+            nc.sync.dma_start(share_col[:], share.rearrange("(p t) o -> p (t o)", t=PACK))
+
+        def load_qs():
+            nc.sync.dma_start(qs_col[:], qs.rearrange("(p t) o -> p (t o)", t=PACK))
+
+        def load_q():
+            nc.sync.dma_start(q_raw[:], query_rows)
+
+        def load_g():
+            nc.sync.dma_start(g_raw[:], grows_rows)
+
+        def load_v(t):
+            nc.sync.dma_start(v_pool[t][:], vals_rows[:, t, :])
+
+        def load_old():
+            nc.sync.dma_start(old_sb[:], old_rows)
+
+        ident = sb.tile([P, P], F32, name="ident")
+        warm = sb.tile([P, 1], F32, name="warm")
+        warm_out = sb.tile([P, 1], F32, name="warm_out")
+        pre_row = sb.tile([P, I], F32, name="pre_row")
+        sg_row = sb.tile([P, I], F32, name="sg_row")
         share16 = sb.tile([P, PACK], F32, name="share16")
         nshare16 = sb.tile([P, PACK], F32, name="nshare16")
-        nc.scalar.activation(out=share16[:], in_=share_col[:], func=ACT.Copy, scale=1.0 / PAGE)
-        nc.scalar.activation(out=nshare16[:], in_=share_col[:], func=ACT.Copy, scale=-1.0 / PAGE)
+
+        def spread(col, row, name):
+            bank = ps.tile([P, 2, P], F32, name=name)
+            for c in range(2):
+                nc.tensor.transpose(bank[:, c, :], col[:, c : c + 1].to_broadcast([P, P]), ident[:])
+            nc.scalar.copy(out=row[:].rearrange("p (n c) -> p n c", c=2), in_=bank[:].rearrange("p c n -> p n c"))
+
+        def shares():
+            nc.scalar.activation(out=nshare16[:], in_=share_col[:], func=ACT.Copy, scale=-1.0 / PAGE)
+            nc.scalar.activation(out=share16[:], in_=share_col[:], func=ACT.Copy, scale=1.0 / PAGE)
 
         k_words = sb.tile([P, I], U32, name="k_words", align_bytes=64)
         k_bytes = sb.tile([P, I], U8, name="k_bytes", align_bytes=64)
-        nc.vector.tensor_copy(k_words[:], key_words[:].bitcast(U32).indirect(offsets[:]))
-        nc.vector.tensor_copy(k_bytes[:], key_bytes[:].indirect(offsets[:]))
-
         q_bf = sb.tile([P, PACK, P, PACK], BF16, name="q_bf", align_bytes=64)
-        deal_cast(nc.scalar.copy, q_bf, q_raw[0], 0)
-        deal_cast(nc.vector.tensor_copy, q_bf, q_raw[1], 1)
         q_codes = sb.tile([P, Q], U32, name="q_codes", align_bytes=64)
         q_scales = sb.tile([P, Q], U8, name="q_scales", align_bytes=64)
-        nc.vector.quantize_mx(
-            out=q_codes[:].bitcast(FP8X4), scales=q_scales[:], in_=q_bf[:].rearrange("p r s j -> p (r s j)")
-        )
+        g_bf = sb.tile([P, PACK, P, PACK], BF16, name="g_bf", align_bytes=64)
+        g_codes = sb.tile([P, E], U32, name="g_codes", align_bytes=64)
+        g_scales = sb.tile([P, E], U8, name="g_scales", align_bytes=64)
+
+        def gather_kw():
+            nc.vector.tensor_copy(k_words[:], key_words[:].bitcast(U32).indirect(offsets[:]))
+
+        def gather_ks():
+            nc.vector.tensor_copy(k_bytes[:], key_bytes[:].indirect(offsets[:]))
+
+        def quantise(codes, scales, grouped):
+            nc.vector.quantize_mx(out=codes[:].bitcast(FP8X4), scales=scales[:], in_=grouped)
 
         neg_max = sb.tile([P, PACK], F32, name="neg_max")
         sums = sb.tile([P, PACK], F32, name="sums")
         probs = sb.tile([P, PACK, I], F32, name="probs")
-        for r in range(PACK):
+        scores = [ps.tile([P, I], F32, name="scores%d" % r) for r in range(PACK)]
+
+        def score(r):
             cols = slice(P * r, P * (r + 1))
-            scores = ps.tile([P, I], F32, name="scores%d" % r)
             nc.tensor.matmul_mx(
-                out=scores[:],
+                out=scores[r][:],
                 lhsT=q_codes[:, cols].bitcast(FP8X4),
                 lhsT_scale=q_scales[:, cols],
                 rhs=k_words[:].bitcast(FP8X4),
@@ -129,45 +145,56 @@ def tile_attend_bvpagecentred_d_pl_kernel(
                 start=True,
                 stop=True,
             )
-            nc.vector.tensor_reduce(out=neg_max[:, r : r + 1], in_=scores[:], axis=AX.X, op=ALU.max, negate=True)
+
+        def row_max(r):
+            nc.vector.tensor_reduce(out=neg_max[:, r : r + 1], in_=scores[r][:], axis=AX.X, op=ALU.max, negate=True)
+
+        def exp(r):
             nc.scalar.activation(
                 out=probs[:, r, :],
-                in_=scores[:],
+                in_=scores[r][:],
                 func=ACT.Exp,
                 bias=neg_max[:, r : r + 1],
                 scale=1.0,
                 accum_out=sums[:, r : r + 1],
             )
 
+        x1 = [sb.tile([P, I], F32, name="x1_%d" % t) for t in range(PACK)]
+        page_sum = [sb.tile([P, G], F32, name="page_sum%d" % t) for t in range(PACK)]
+        x2 = [sb.tile([P, I], F32, name="x2_%d" % t) for t in range(PACK)]
+        vp = [sb.tile([P, I], F32, name="vp_%d" % t) for t in range(PACK)]
         sq = sb.tile([P, PACK, I], F32, name="sq")
 
-        def prepare_plane(t):
-            x1 = sb.tile([P, I], F32, name="x1_%d" % t)
-            nc.vector.tensor_tensor(x1[:], v_pool[t][:].indirect(offsets[:]), pre_row[:], ALU.mult)
-            page_sum = sb.tile([P, G], F32, name="page_sum%d" % t)
-            nc.vector.tensor_reduce(
-                out=page_sum[:], in_=x1[:].rearrange("p (g k) -> p g k", k=PAGE), axis=AX.X, op=ALU.add
-            )
-            x2 = sb.tile([P, I], F32, name="x2_%d" % t)
+        def gather_v(t):
+            nc.vector.tensor_tensor(x1[t][:], v_pool[t][:].indirect(offsets[:]), pre_row[:], ALU.mult)
+
+        def sum_pages(t):
+            nc.vector.tensor_reduce(out=page_sum[t][:], in_=paged(x1[t][:]), axis=AX.X, op=ALU.add)
+
+        def centre(t):
             nc.vector.scalar_tensor_tensor(
-                out=x2[:].rearrange("p (g k) -> p g k", k=PAGE),
-                in0=page_sum[:].unsqueeze(2).to_broadcast([P, G, PAGE]),
+                out=paged(x2[t][:]),
+                in0=page_sum[t][:].unsqueeze(2).to_broadcast([P, G, PAGE]),
                 scalar=nshare16[:, t : t + 1],
-                in1=x1[:].rearrange("p (g k) -> p g k", k=PAGE),
+                in1=paged(x1[t][:]),
                 op0=ALU.mult,
                 op1=ALU.add,
             )
-            vp = sb.tile([P, I], F32, name="vp_%d" % t)
-            nc.scalar.activation(out=vp[:], in_=x2[:], func=ACT.Tanh)
-            nc.scalar.activation(out=sq[:, t, :], in_=vp[:], func=ACT.Square)
 
-        prepare_plane(0)
-        prepare_plane(1)
+        def tanh_sq(t):
+            nc.scalar.activation(out=vp[t][:], in_=x2[t][:], func=ACT.Tanh)
+            nc.scalar.activation(out=sq[:, t, :], in_=vp[t][:], func=ACT.Square)
 
         inv = sb.tile([P, PACK], F32, name="inv")
-        nc.vector.reciprocal(out=inv[:], in_=sums[:])
         w_planes = sb.tile([P, PACK, I], BF16, name="w_planes", align_bytes=64)
-        for r in range(PACK):
+        w_bf = sb.tile([P, I, PACK], BF16, name="w_bf", align_bytes=64)
+        w_codes = sb.tile([P, I], U32, name="w_codes", align_bytes=64)
+        w_scales = sb.tile([P, I], U8, name="w_scales", align_bytes=64)
+
+        def invert():
+            nc.vector.reciprocal(out=inv[:], in_=sums[:])
+
+        def weigh(r):
             nc.vector.tensor_scalar(
                 out=w_planes[:, r, :],
                 in0=probs[:, r, :],
@@ -176,100 +203,173 @@ def tile_attend_bvpagecentred_d_pl_kernel(
                 op0=ALU.mult,
                 op1=ALU.mult,
             )
-        w_bf = sb.tile([P, I, PACK], BF16, name="w_bf", align_bytes=64)
-        nc.vector.tensor_copy(
-            out=w_bf[:].rearrange("p (c i) r -> p c r i", i=4),
-            in_=w_planes[:].rearrange("p r (c i) -> p c r i", i=4),
-        )
-        w_codes = sb.tile([P, I], U32, name="w_codes", align_bytes=64)
-        w_scales = sb.tile([P, I], U8, name="w_scales", align_bytes=64)
-        nc.vector.quantize_mx(
-            out=w_codes[:].bitcast(FP8X4), scales=w_scales[:], in_=w_bf[:].rearrange("p i r -> p (i r)")
-        )
 
-        g_bf = sb.tile([P, PACK, P, PACK], BF16, name="g_bf", align_bytes=64)
-        deal_cast(nc.scalar.copy, g_bf, g_raw[0], 0)
-        deal_cast(nc.scalar.copy, g_bf, g_raw[1], 1)
-        g_codes = sb.tile([P, E], U32, name="g_codes", align_bytes=64)
-        g_scales = sb.tile([P, E], U8, name="g_scales", align_bytes=64)
-        nc.vector.quantize_mx(
-            out=g_codes[:].bitcast(FP8X4), scales=g_scales[:], in_=g_bf[:].rearrange("p r s j -> p (r s j)")
-        )
+        def weave_w():
+            nc.vector.tensor_copy(
+                out=w_bf[:].rearrange("p (c i) r -> p c r i", i=4),
+                in_=w_planes[:].rearrange("p r (c i) -> p c r i", i=4),
+            )
 
-        c0 = [ps.tile([P, PACK, HALF], F32, name="c0_%d" % h) for h in range(2)]
-        for h in range(2):
-            slots = slice(HALF * h, HALF * (h + 1))
-            for t in range(PACK):
-                cols = slice(P * t, P * (t + 1))
-                nc.tensor.matmul_mx(
-                    out=c0[h][:, t, :],
-                    lhsT=g_codes[:, cols].bitcast(FP8X4),
-                    lhsT_scale=g_scales[:, cols],
-                    rhs=w_codes[:, slots].bitcast(FP8X4),
-                    rhs_scale=w_scales[:, slots],
-                    start=True,
-                    stop=True,
-                )
+        c0 = [ps.tile([P, 2, I], F32, name="c0_%d" % u) for u in range(2)]
 
-        prepare_plane(2)
-        prepare_plane(3)
+        def grad(t):
+            cols = slice(P * t, P * (t + 1))
+            nc.tensor.matmul_mx(
+                out=c0[t // 2][:, t % 2, :],
+                lhsT=g_codes[:, cols].bitcast(FP8X4),
+                lhsT_scale=g_scales[:, cols],
+                rhs=w_codes[:].bitcast(FP8X4),
+                rhs_scale=w_scales[:],
+                start=True,
+                stop=True,
+            )
 
-        halves = [slice(HALF * h, HALF * (h + 1)) for h in range(2)]
-        ndx2 = [sb.tile([P, PACK, HALF], F32, name="ndx2_%d" % h) for h in range(2)]
-        back_sum = [sb.tile([P, PACK, G // 2], F32, name="back_sum%d" % h) for h in range(2)]
-        dx1 = [sb.tile([P, PACK, HALF], F32, name="dx1_%d" % h) for h in range(2)]
-        gained = [sb.tile([P, PACK, HALF], F32, name="gained%d" % h) for h in range(2)]
-        y = [sb.tile([P, PACK, HALF], F32, name="y%d" % h) for h in range(2)]
-        y_bf = [sb.tile([P, HALF, PACK], BF16, name="y_bf%d" % h, align_bytes=64) for h in range(2)]
+        ndx2 = sb.tile([P, PACK, I], F32, name="ndx2")
+        back_sum = sb.tile([P, PACK, G], F32, name="back_sum")
+        dx1 = sb.tile([P, PACK, I], F32, name="dx1")
+        gained = sb.tile([P, PACK, I], F32, name="gained")
+        y = sb.tile([P, PACK, I], F32, name="y")
+        y_bf = sb.tile([P, I, PACK], BF16, name="y_bf", align_bytes=64)
         y_codes = sb.tile([P, I], U32, name="y_codes", align_bytes=64)
         y_scales = sb.tile([P, I], U8, name="y_scales", align_bytes=64)
-        for h in range(2):
+
+        def through_tanh(t0, t1):
             nc.vector.scalar_tensor_tensor(
-                out=ndx2[h][:], in0=sq[:, :, halves[h]], scalar=1.0, in1=c0[h][:], op0=ALU.subtract, op1=ALU.mult
+                out=ndx2[:, t0:t1, :],
+                in0=sq[:, t0:t1, :],
+                scalar=1.0,
+                in1=c0[t0 // 2][:, t0 % 2 : t0 % 2 + t1 - t0, :],
+                op0=ALU.subtract,
+                op1=ALU.mult,
             )
-        for h in range(2):
+
+        def sum_back(t0, t1):
             nc.vector.tensor_reduce(
-                out=back_sum[h][:].rearrange("p t g -> p (t g)"),
-                in_=ndx2[h][:].rearrange("p t (g k) -> p (t g) k", k=PAGE),
+                out=back_sum[:, t0:t1, :].rearrange("p t g -> p (t g)"),
+                in_=paged(ndx2[:, t0:t1, :].rearrange("p t i -> p (t i)")),
                 axis=AX.X,
                 op=ALU.add,
             )
-        for h in range(2):
-            for t in range(PACK):
-                nc.vector.scalar_tensor_tensor(
-                    out=dx1[h][:, t, :].rearrange("p (g k) -> p g k", k=PAGE),
-                    in0=back_sum[h][:, t, :].unsqueeze(2).to_broadcast([P, G // 2, PAGE]),
-                    scalar=share16[:, t : t + 1],
-                    in1=ndx2[h][:, t, :].rearrange("p (g k) -> p g k", k=PAGE),
-                    op0=ALU.mult,
-                    op1=ALU.subtract,
-                )
-        for h in range(2):
+
+        def through_mean(t):
+            nc.vector.scalar_tensor_tensor(
+                out=paged(dx1[:, t, :]),
+                in0=back_sum[:, t, :].unsqueeze(2).to_broadcast([P, G, PAGE]),
+                scalar=share16[:, t : t + 1],
+                in1=paged(ndx2[:, t, :]),
+                op0=ALU.mult,
+                op1=ALU.subtract,
+            )
+
+        def gain(t0, t1):
             nc.vector.tensor_tensor(
-                out=gained[h][:],
-                in0=dx1[h][:],
-                in1=sg_row[:, halves[h]].unsqueeze(1).to_broadcast([P, PACK, HALF]),
+                out=gained[:, t0:t1, :],
+                in0=dx1[:, t0:t1, :],
+                in1=sg_row[:].unsqueeze(1).to_broadcast([P, t1 - t0, I]),
                 op=ALU.mult,
             )
-        out_rows = out_0.rearrange("(p t) i -> p t i", t=PACK)
-        for h in range(2):
-            nc.vector.tensor_tensor(out=y[h][:], in0=gained[h][:], in1=old_sb[:, :, halves[h]], op=ALU.add)
-            nc.sync.dma_start(out_rows[:, :, halves[h]], y[h][:])
-        for h, engine_copy in ((0, nc.scalar.copy), (1, nc.vector.tensor_copy)):
+
+        def add_old(t0, t1, engine):
+            engine.tensor_tensor(out=y[:, t0:t1, :], in0=gained[:, t0:t1, :], in1=old_sb[:, t0:t1, :], op=ALU.add)
+
+        def store_y(t0, t1):
+            nc.sync.dma_start(out_rows[:, t0:t1, :], y[:, t0:t1, :])
+
+        def round_y(engine_copy, i0, i1):
             engine_copy(
-                out=y_bf[h][:].rearrange("p (c i) t -> p c t i", i=4),
-                in_=y[h][:].rearrange("p t (c i) -> p c t i", i=4),
+                out=y_bf[:, i0:i1, :].rearrange("p (c i) t -> p c t i", i=4),
+                in_=y[:, :, i0:i1].rearrange("p t (c i) -> p c t i", i=4),
             )
-        for h in range(2):
-            nc.vector.quantize_mx(
-                out=y_codes[:, halves[h]].bitcast(FP8X4),
-                scales=y_scales[:, halves[h]],
-                in_=y_bf[h][:].rearrange("p i t -> p (i t)"),
-            )
-        nc.sync.dma_start(out_1[0].rearrange("p n t -> p (n t)").bitcast(I32), y_codes[:].bitcast(I32))
-        for quad in range(4):
-            queue = nc.sync if quad % 2 == 0 else nc.scalar
-            queue.dma_start(
-                out_2[0, 4 * quad : 4 * quad + 4, :].bitcast(I32),
-                y_scales[32 * quad : 32 * quad + 4, :].bitcast(I32),
-            )
+
+        def store_planes():
+            nc.sync.dma_start(out_1[0].rearrange("p n t -> p (n t)").bitcast(I32), y_codes[:].bitcast(I32))
+            for quad in range(4):
+                queue = nc.scalar if quad % 2 == 0 else nc.sync
+                queue.dma_start(
+                    out_2[0, 4 * quad : 4 * quad + 4, :].bitcast(I32),
+                    y_scales[32 * quad : 32 * quad + 4, :].bitcast(I32),
+                )
+
+        def clock(ap, name):
+            tick = sb.tile([P, 1], F32, name=name)
+            nc.gpsimd.tensor_copy(out=tick[:], in_=ap)
+
+        nc.gpsimd.memset(key_bytes[:].bitcast(I32), 0)
+        load_offs()
+        load_pre()
+        load_kw()
+        load_ks()
+        load_v(0)
+        load_q()
+        load_share()
+        load_v(1)
+        load_g()
+        load_qs()
+        load_sg()
+        load_v(2)
+        load_v(3)
+        load_old()
+        nc.vector.memset(warm[:], 0.0)
+        nc.scalar.activation(out=warm_out[:], in_=warm[:], func=ACT.Exp)
+        make_identity(nc, ident[:])
+        spread(pre_col, pre_row, "pre_bank")
+        shares()
+        gather_kw()
+        gather_v(0)
+        gather_ks()
+        sum_pages(0)
+        centre(0)
+        deal_cast(nc.scalar.copy, q_bf, q_raw, 0, 48)
+        deal_cast(nc.vector.tensor_copy, q_bf, q_raw, 48, 128)
+        quantise(q_codes, q_scales, q_bf[:].rearrange("p r s j -> p (r s j)"))
+        tanh_sq(0)
+        for r in range(PACK):
+            score(r)
+        gather_v(1)
+        for r in range(PACK):
+            row_max(r)
+            exp(r)
+        deal_cast(nc.scalar.copy, g_bf, g_raw, 0, 64)
+        deal_cast(nc.scalar.copy, g_bf, g_raw, 64, 128)
+        sum_pages(1)
+        invert()
+        centre(1)
+        for r in range(PACK):
+            weigh(r)
+        gather_v(2)
+        weave_w()
+        sum_pages(2)
+        quantise(w_codes, w_scales, w_bf[:].rearrange("p i r -> p (i r)"))
+        centre(2)
+        quantise(g_codes, g_scales, g_bf[:].rearrange("p r s j -> p (r s j)"))
+        tanh_sq(1)
+        for t in range(PACK):
+            grad(t)
+        spread(sg_col, sg_row, "sg_bank")
+        tanh_sq(2)
+        gather_v(3)
+        through_tanh(0, 2)
+        sum_pages(3)
+        sum_back(0, 2)
+        centre(3)
+        tanh_sq(3)
+        through_mean(0)
+        through_mean(1)
+        through_tanh(2, 3)
+        gain(0, 2)
+        add_old(0, 2, nc.gpsimd)
+        store_y(0, 2)
+        through_tanh(3, 4)
+        sum_back(2, 3)
+        sum_back(3, 4)
+        through_mean(2)
+        through_mean(3)
+        gain(2, 3)
+        gain(3, 4)
+        add_old(2, 3, nc.vector)
+        add_old(3, 4, nc.vector)
+        store_y(2, 4)
+        round_y(nc.scalar.copy, 0, 96)
+        round_y(nc.vector.tensor_copy, 96, 256)
+        quantise(y_codes, y_scales, y_bf[:].rearrange("p i t -> p (i t)"))
+        store_planes()

@@ -30,10 +30,18 @@ def tile_attend_bvpagecentred_d_pl_kernel(
         sb = ctx.enter_context(tc.tile_pool(name="sb", bufs=1))
         ps = ctx.enter_context(tc.psum_pool(name="ps", bufs=1))
 
-        def deal_cast(engine_copy, grouped, raw, s0, s1):
+        def deal_cast(engine_copy, grouped, raw, u):
             engine_copy(
-                out=grouped[:, :, s0:s1, :].rearrange("p r s j -> p s r j"),
-                in_=raw[:, :, PACK * s0 : PACK * s1].rearrange("p j (s r) -> p s r j", r=PACK),
+                out=grouped[:, 2 * u : 2 * u + 2, :, :].rearrange("p r s j -> p s j r"),
+                in_=raw[:].rearrange("p j (s r) -> p s j r", r=PACK)[:, :, :, 2 * u : 2 * u + 2],
+            )
+
+        def quantise_pair(codes, scales, grouped, u):
+            cols = slice(2 * P * u, 2 * P * (u + 1))
+            nc.vector.quantize_mx(
+                out=codes[:, cols].bitcast(FP8X4),
+                scales=scales[:, cols],
+                in_=grouped[:, 2 * u : 2 * u + 2, :, :].rearrange("p r s j -> p (r s j)"),
             )
 
         def paged(ap):
@@ -191,8 +199,8 @@ def tile_attend_bvpagecentred_d_pl_kernel(
         w_codes = sb.tile([P, I], U32, name="w_codes", align_bytes=64)
         w_scales = sb.tile([P, I], U8, name="w_scales", align_bytes=64)
 
-        def invert():
-            nc.vector.reciprocal(out=inv[:], in_=sums[:])
+        def invert(u):
+            nc.vector.reciprocal(out=inv[:, 2 * u : 2 * u + 2], in_=sums[:, 2 * u : 2 * u + 2])
 
         def weigh(r):
             nc.vector.tensor_scalar(
@@ -300,12 +308,12 @@ def tile_attend_bvpagecentred_d_pl_kernel(
         load_kw()
         load_ks()
         load_v(0)
-        load_q()
-        load_share()
         load_v(1)
-        load_g()
+        load_share()
+        load_q()
         load_qs()
         load_sg()
+        load_g()
         load_v(2)
         load_v(3)
         load_old()
@@ -318,41 +326,50 @@ def tile_attend_bvpagecentred_d_pl_kernel(
         gather_v(0)
         gather_ks()
         sum_pages(0)
-        centre(0)
-        deal_cast(nc.scalar.copy, q_bf, q_raw, 0, 48)
-        deal_cast(nc.vector.tensor_copy, q_bf, q_raw, 48, 128)
-        quantise(q_codes, q_scales, q_bf[:].rearrange("p r s j -> p (r s j)"))
-        tanh_sq(0)
-        for r in range(PACK):
-            score(r)
         gather_v(1)
+        centre(0)
+        sum_pages(1)
+        tanh_sq(0)
+        deal_cast(nc.vector.tensor_copy, q_bf, q_raw, 0)
+        deal_cast(nc.scalar.copy, q_bf, q_raw, 1)
+        centre(1)
+        quantise_pair(q_codes, q_scales, q_bf, 0)
+        score(0)
+        score(1)
+        quantise_pair(q_codes, q_scales, q_bf, 1)
+        score(2)
+        score(3)
+        tanh_sq(1)
+        spread(sg_col, sg_row, "sg_bank")
         for r in range(PACK):
             row_max(r)
             exp(r)
-        deal_cast(nc.scalar.copy, g_bf, g_raw, 0, 64)
-        deal_cast(nc.scalar.copy, g_bf, g_raw, 64, 128)
-        sum_pages(1)
-        invert()
-        centre(1)
-        for r in range(PACK):
-            weigh(r)
+        deal_cast(nc.scalar.copy, g_bf, g_raw, 0)
+        invert(0)
         gather_v(2)
-        weave_w()
+        weigh(0)
+        invert(1)
+        weigh(1)
         sum_pages(2)
-        quantise(w_codes, w_scales, w_bf[:].rearrange("p i r -> p (i r)"))
+        weigh(2)
+        weigh(3)
         centre(2)
-        quantise(g_codes, g_scales, g_bf[:].rearrange("p r s j -> p (r s j)"))
-        tanh_sq(1)
-        for t in range(PACK):
-            grad(t)
-        spread(sg_col, sg_row, "sg_bank")
+        weave_w()
+        quantise_pair(g_codes, g_scales, g_bf, 0)
+        quantise(w_codes, w_scales, w_bf[:].rearrange("p i r -> p (i r)"))
+        grad(0)
+        grad(1)
+        deal_cast(nc.scalar.copy, g_bf, g_raw, 1)
         tanh_sq(2)
         gather_v(3)
-        through_tanh(0, 2)
+        quantise_pair(g_codes, g_scales, g_bf, 1)
+        grad(2)
+        grad(3)
         sum_pages(3)
-        sum_back(0, 2)
+        through_tanh(0, 2)
         centre(3)
         tanh_sq(3)
+        sum_back(0, 2)
         through_mean(0)
         through_mean(1)
         through_tanh(2, 3)

from contextlib import ExitStack

import concourse.mybir as mybir
from concourse.masks import make_identity

D, E, T, I, Q, G = 512, 512, 1024, 256, 512, 16
FLOPS = 2 * D * Q * I + 2 * Q * E * I

F32 = mybir.dt.float32
BF16 = mybir.dt.bfloat16
I32 = mybir.dt.int32
U32 = mybir.dt.uint32
U16 = mybir.dt.uint16
U8 = mybir.dt.uint8
FP8X4 = mybir.dt.float8_e4m3fn_x4
ALU = mybir.AluOpType
ACT = mybir.ActivationFunctionType
AX = mybir.AxisListType

P = 128
PACK = 4
PAGE = I // G


def tile_attend_bvpagecentred_d_pl_kernel(
    tc, query, qs, grows, vals, keys_words, keys_scales, share, pre, sg, old, offs, out_0, out_1, out_2
):
    nc = tc.nc
    with ExitStack() as ctx:
        sb = ctx.enter_context(tc.tile_pool(name="sb", bufs=1))
        ps = ctx.enter_context(tc.psum_pool(name="ps", bufs=1))

        def deal_cast(engine_copy, grouped, raw, u):
            engine_copy(
                out=grouped[:, 2 * u : 2 * u + 2, :, :].rearrange("p r s j -> p s j r"),
                in_=raw[:].rearrange("p j (s r) -> p s j r", r=PACK)[:, :, :, 2 * u : 2 * u + 2],
            )

        def quantise_pair(codes, scales, grouped, u):
            cols = slice(2 * P * u, 2 * P * (u + 1))
            nc.vector.quantize_mx(
                out=codes[:, cols].bitcast(FP8X4),
                scales=scales[:, cols],
                in_=grouped[:, 2 * u : 2 * u + 2, :, :].rearrange("p r s j -> p (r s j)"),
            )

        def paged(ap):
            return ap.rearrange("p (g k) -> p g k", k=PAGE)

        offsets = sb.tile([P, I // 16], U16, name="offsets")
        key_words = sb.tile([P, T], I32, name="key_words", align_bytes=64)
        key_bytes = sb.tile([P, T], U8, name="key_bytes", align_bytes=64)
        pre_col = sb.tile([P, 2], F32, name="pre_col")
        share_col = sb.tile([P, PACK], F32, name="share_col")
        sg_col = sb.tile([P, 2], F32, name="sg_col")
        qs_col = sb.tile([P, PACK], F32, name="qs_col")
        query_rows = query.rearrange("(p j) q -> p j q", j=PACK)
        grows_rows = grows.rearrange("(p j) e -> p j e", j=PACK)
        vals_rows = vals.rearrange("(p t) n -> p t n", t=PACK)
        old_rows = old.rearrange("(p t) i -> p t i", t=PACK)
        out_rows = out_0.rearrange("(p t) i -> p t i", t=PACK)
        q_raw = sb.tile([P, PACK, Q], F32, name="q_raw")
        g_raw = sb.tile([P, PACK, E], F32, name="g_raw")
        v_pool = [sb.tile([P, T], F32, name="v_pool%d" % t) for t in range(PACK)]
        old_sb = sb.tile([P, PACK, I], F32, name="old_sb")

        def load_offs():
            nc.sync.dma_start(offsets[:], offs)

        def load_kw():
            nc.sync.dma_start(key_words[:], keys_words[0].rearrange("p n t -> p (n t)").bitcast(I32))

        def load_ks():
            for quad in range(4):
                nc.sync.dma_start(
                    key_bytes[32 * quad : 32 * quad + 4, :].bitcast(I32),
                    keys_scales[0, 4 * quad : 4 * quad + 4, :].bitcast(I32),
                )

        def load_pre():
            nc.sync.dma_start(pre_col[:], pre.rearrange("o (p c) -> (o p) c", c=2))

        def load_sg():
            nc.sync.dma_start(sg_col[:], sg.rearrange("o (p c) -> (o p) c", c=2))

        def load_share():
            nc.sync.dma_start(share_col[:], share.rearrange("(p t) o -> p (t o)", t=PACK))

        def load_qs():
            nc.sync.dma_start(qs_col[:], qs.rearrange("(p t) o -> p (t o)", t=PACK))

        def load_q():
            nc.sync.dma_start(q_raw[:], query_rows)

        def load_g():
            nc.sync.dma_start(g_raw[:], grows_rows)

        def load_v(t):
            nc.sync.dma_start(v_pool[t][:], vals_rows[:, t, :])

        def load_old():
            nc.sync.dma_start(old_sb[:], old_rows)

        ident = sb.tile([P, P], F32, name="ident")
        warm = sb.tile([P, 1], F32, name="warm")
        warm_out = sb.tile([P, 1], F32, name="warm_out")
        pre_row = sb.tile([P, I], F32, name="pre_row")
        sg_row = sb.tile([P, I], F32, name="sg_row")
        share16 = sb.tile([P, PACK], F32, name="share16")
        nshare16 = sb.tile([P, PACK], F32, name="nshare16")

        def spread(col, row, name):
            bank = ps.tile([P, 2, P], F32, name=name)
            for c in range(2):
                nc.tensor.transpose(bank[:, c, :], col[:, c : c + 1].to_broadcast([P, P]), ident[:])
            nc.scalar.copy(out=row[:].rearrange("p (n c) -> p n c", c=2), in_=bank[:].rearrange("p c n -> p n c"))

        def shares():
            nc.scalar.activation(out=nshare16[:], in_=share_col[:], func=ACT.Copy, scale=-1.0 / PAGE)
            nc.scalar.activation(out=share16[:], in_=share_col[:], func=ACT.Copy, scale=1.0 / PAGE)

        k_words = sb.tile([P, I], U32, name="k_words", align_bytes=64)
        k_bytes = sb.tile([P, I], U8, name="k_bytes", align_bytes=64)
        q_bf = sb.tile([P, PACK, P, PACK], BF16, name="q_bf", align_bytes=64)
        q_codes = sb.tile([P, Q], U32, name="q_codes", align_bytes=64)
        q_scales = sb.tile([P, Q], U8, name="q_scales", align_bytes=64)
        g_bf = sb.tile([P, PACK, P, PACK], BF16, name="g_bf", align_bytes=64)
        g_codes = sb.tile([P, E], U32, name="g_codes", align_bytes=64)
        g_scales = sb.tile([P, E], U8, name="g_scales", align_bytes=64)

        def gather_kw():
            nc.vector.tensor_copy(k_words[:], key_words[:].bitcast(U32).indirect(offsets[:]))

        def gather_ks():
            nc.vector.tensor_copy(k_bytes[:], key_bytes[:].indirect(offsets[:]))

        def quantise(codes, scales, grouped):
            nc.vector.quantize_mx(out=codes[:].bitcast(FP8X4), scales=scales[:], in_=grouped)

        neg_max = sb.tile([P, PACK], F32, name="neg_max")
        sums = sb.tile([P, PACK], F32, name="sums")
        probs = sb.tile([P, PACK, I], F32, name="probs")
        scores = [ps.tile([P, I], F32, name="scores%d" % r) for r in range(PACK)]

        def score(r):
            cols = slice(P * r, P * (r + 1))
            nc.tensor.matmul_mx(
                out=scores[r][:],
                lhsT=q_codes[:, cols].bitcast(FP8X4),
                lhsT_scale=q_scales[:, cols],
                rhs=k_words[:].bitcast(FP8X4),
                rhs_scale=k_bytes[:],
                start=True,
                stop=True,
            )

        def row_max(r):
            nc.vector.tensor_reduce(out=neg_max[:, r : r + 1], in_=scores[r][:], axis=AX.X, op=ALU.max, negate=True)

        def exp(r):
            nc.scalar.activation(
                out=probs[:, r, :],
                in_=scores[r][:],
                func=ACT.Exp,
                bias=neg_max[:, r : r + 1],
                scale=1.0,
                accum_out=sums[:, r : r + 1],
            )

        x1 = [sb.tile([P, I], F32, name="x1_%d" % t) for t in range(PACK)]
        page_sum = [sb.tile([P, G], F32, name="page_sum%d" % t) for t in range(PACK)]
        x2 = [sb.tile([P, I], F32, name="x2_%d" % t) for t in range(PACK)]
        vp = [sb.tile([P, I], F32, name="vp_%d" % t) for t in range(PACK)]
        sq = sb.tile([P, PACK, I], F32, name="sq")

        def gather_v(t):
            nc.vector.tensor_tensor(x1[t][:], v_pool[t][:].indirect(offsets[:]), pre_row[:], ALU.mult)

        def sum_pages(t):
            nc.vector.tensor_reduce(out=page_sum[t][:], in_=paged(x1[t][:]), axis=AX.X, op=ALU.add)

        def centre(t):
            nc.vector.scalar_tensor_tensor(
                out=paged(x2[t][:]),
                in0=page_sum[t][:].unsqueeze(2).to_broadcast([P, G, PAGE]),
                scalar=nshare16[:, t : t + 1],
                in1=paged(x1[t][:]),
                op0=ALU.mult,
                op1=ALU.add,
            )

        def tanh_sq(t):
            nc.scalar.activation(out=vp[t][:], in_=x2[t][:], func=ACT.Tanh)
            nc.scalar.activation(out=sq[:, t, :], in_=vp[t][:], func=ACT.Square)

        inv = sb.tile([P, PACK], F32, name="inv")
        w_planes = sb.tile([P, PACK, I], BF16, name="w_planes", align_bytes=64)
        w_bf = sb.tile([P, I, PACK], BF16, name="w_bf", align_bytes=64)
        w_codes = sb.tile([P, I], U32, name="w_codes", align_bytes=64)
        w_scales = sb.tile([P, I], U8, name="w_scales", align_bytes=64)

        def invert(u):
            nc.vector.reciprocal(out=inv[:, 2 * u : 2 * u + 2], in_=sums[:, 2 * u : 2 * u + 2])

        def weigh(r):
            nc.vector.tensor_scalar(
                out=w_planes[:, r, :],
                in0=probs[:, r, :],
                scalar1=qs_col[:, r : r + 1],
                scalar2=inv[:, r : r + 1],
                op0=ALU.mult,
                op1=ALU.mult,
            )

        def weave_w():
            nc.vector.tensor_copy(
                out=w_bf[:].rearrange("p (c i) r -> p c r i", i=4),
                in_=w_planes[:].rearrange("p r (c i) -> p c r i", i=4),
            )

        c0 = [ps.tile([P, 2, I], F32, name="c0_%d" % u) for u in range(2)]

        def grad(t):
            cols = slice(P * t, P * (t + 1))
            nc.tensor.matmul_mx(
                out=c0[t // 2][:, t % 2, :],
                lhsT=g_codes[:, cols].bitcast(FP8X4),
                lhsT_scale=g_scales[:, cols],
                rhs=w_codes[:].bitcast(FP8X4),
                rhs_scale=w_scales[:],
                start=True,
                stop=True,
            )

        ndx2 = sb.tile([P, PACK, I], F32, name="ndx2")
        back_sum = sb.tile([P, PACK, G], F32, name="back_sum")
        dx1 = sb.tile([P, PACK, I], F32, name="dx1")
        gained = sb.tile([P, PACK, I], F32, name="gained")
        y = sb.tile([P, PACK, I], F32, name="y")
        y_bf = sb.tile([P, I, PACK], BF16, name="y_bf", align_bytes=64)
        y_codes = sb.tile([P, I], U32, name="y_codes", align_bytes=64)
        y_scales = sb.tile([P, I], U8, name="y_scales", align_bytes=64)

        def through_tanh(t0, t1):
            nc.vector.scalar_tensor_tensor(
                out=ndx2[:, t0:t1, :],
                in0=sq[:, t0:t1, :],
                scalar=1.0,
                in1=c0[t0 // 2][:, t0 % 2 : t0 % 2 + t1 - t0, :],
                op0=ALU.subtract,
                op1=ALU.mult,
            )

        def sum_back(t0, t1):
            nc.vector.tensor_reduce(
                out=back_sum[:, t0:t1, :].rearrange("p t g -> p (t g)"),
                in_=paged(ndx2[:, t0:t1, :].rearrange("p t i -> p (t i)")),
                axis=AX.X,
                op=ALU.add,
            )

        def through_mean(t):
            nc.vector.scalar_tensor_tensor(
                out=paged(dx1[:, t, :]),
                in0=back_sum[:, t, :].unsqueeze(2).to_broadcast([P, G, PAGE]),
                scalar=share16[:, t : t + 1],
                in1=paged(ndx2[:, t, :]),
                op0=ALU.mult,
                op1=ALU.subtract,
            )

        def gain(t0, t1):
            nc.vector.tensor_tensor(
                out=gained[:, t0:t1, :],
                in0=dx1[:, t0:t1, :],
                in1=sg_row[:].unsqueeze(1).to_broadcast([P, t1 - t0, I]),
                op=ALU.mult,
            )

        def add_old(t0, t1, engine):
            engine.tensor_tensor(out=y[:, t0:t1, :], in0=gained[:, t0:t1, :], in1=old_sb[:, t0:t1, :], op=ALU.add)

        def store_y(t0, t1):
            nc.sync.dma_start(out_rows[:, t0:t1, :], y[:, t0:t1, :])

        def round_y(engine_copy, i0, i1):
            engine_copy(
                out=y_bf[:, i0:i1, :].rearrange("p (c i) t -> p c t i", i=4),
                in_=y[:, :, i0:i1].rearrange("p t (c i) -> p c t i", i=4),
            )

        def store_planes():
            nc.sync.dma_start(out_1[0].rearrange("p n t -> p (n t)").bitcast(I32), y_codes[:].bitcast(I32))
            for quad in range(4):
                queue = nc.scalar if quad % 2 == 0 else nc.sync
                queue.dma_start(
                    out_2[0, 4 * quad : 4 * quad + 4, :].bitcast(I32),
                    y_scales[32 * quad : 32 * quad + 4, :].bitcast(I32),
                )

        def clock(ap, name):
            tick = sb.tile([P, 1], F32, name=name)
            nc.gpsimd.tensor_copy(out=tick[:], in_=ap)

        nc.gpsimd.memset(key_bytes[:].bitcast(I32), 0)
        load_offs()
        load_pre()
        load_kw()
        load_ks()
        load_v(0)
        load_v(1)
        load_share()
        load_q()
        load_qs()
        load_sg()
        load_g()
        load_v(2)
        load_v(3)
        load_old()
        nc.vector.memset(warm[:], 0.0)
        nc.scalar.activation(out=warm_out[:], in_=warm[:], func=ACT.Exp)
        make_identity(nc, ident[:])
        spread(pre_col, pre_row, "pre_bank")
        shares()
        gather_kw()
        gather_v(0)
        gather_ks()
        sum_pages(0)
        gather_v(1)
        centre(0)
        sum_pages(1)
        tanh_sq(0)
        deal_cast(nc.vector.tensor_copy, q_bf, q_raw, 0)
        deal_cast(nc.scalar.copy, q_bf, q_raw, 1)
        centre(1)
        quantise_pair(q_codes, q_scales, q_bf, 0)
        score(0)
        score(1)
        quantise_pair(q_codes, q_scales, q_bf, 1)
        score(2)
        score(3)
        tanh_sq(1)
        spread(sg_col, sg_row, "sg_bank")
        for r in range(PACK):
            row_max(r)
            exp(r)
        deal_cast(nc.scalar.copy, g_bf, g_raw, 0)
        invert(0)
        gather_v(2)
        weigh(0)
        invert(1)
        weigh(1)
        sum_pages(2)
        weigh(2)
        weigh(3)
        centre(2)
        weave_w()
        quantise_pair(g_codes, g_scales, g_bf, 0)
        quantise(w_codes, w_scales, w_bf[:].rearrange("p i r -> p (i r)"))
        grad(0)
        grad(1)
        deal_cast(nc.scalar.copy, g_bf, g_raw, 1)
        tanh_sq(2)
        gather_v(3)
        quantise_pair(g_codes, g_scales, g_bf, 1)
        grad(2)
        grad(3)
        sum_pages(3)
        through_tanh(0, 2)
        centre(3)
        tanh_sq(3)
        sum_back(0, 2)
        through_mean(0)
        through_mean(1)
        through_tanh(2, 3)
        gain(0, 2)
        add_old(0, 2, nc.gpsimd)
        store_y(0, 2)
        through_tanh(3, 4)
        sum_back(2, 3)
        sum_back(3, 4)
        through_mean(2)
        through_mean(3)
        gain(2, 3)
        gain(3, 4)
        add_old(2, 3, nc.vector)
        add_old(3, 4, nc.vector)
        store_y(2, 4)
        round_y(nc.scalar.copy, 0, 96)
        round_y(nc.vector.tensor_copy, 96, 256)
        quantise(y_codes, y_scales, y_bf[:].rearrange("p i t -> p (i t)"))
        store_planes()
